import numpy as np
import ml_dtypes

BF16 = ml_dtypes.bfloat16


def bf(x):
    return np.asarray(x, np.float32).astype(BF16)


def f32(x):
    return np.asarray(x, np.float32)


def f64(x):
    return np.asarray(x).astype(np.float64)


def striped(idx):
    return np.tile(idx.reshape(-1, 16).T, (8, 1))


S, K, M, N, B, Q = 256, 512, 128, 192, 2, 96


def setup_inputs():
    return {"base": bf(np.random.standard_normal((B, M, S))), "x": bf(np.random.standard_normal((K, N))), "w": bf(np.random.standard_normal((K, M)) / np.sqrt(K)), "b": f32(0.5 * np.random.standard_normal((M, 1))), "offs": striped(np.random.permutation(S)[:N])}


def reference(base, x, w, b, offs):
    idx = offs[:16].T.reshape(-1)
    z = f64(base).copy()
    for i in range(B):
        z[i][:, idx[i * Q : (i + 1) * Q]] += f64(w).T @ f64(x)[:, i * Q : (i + 1) * Q]
    return np.maximum(z + f64(b), 0.0)

@@ -1,0 +1,60 @@
+from concourse.masks import make_identity
+import concourse.mybir as mybir
+
+BF16 = mybir.dt.bfloat16
+F32 = mybir.dt.float32
+U16 = mybir.dt.uint16
+
+P = 128
+FLOPS = 2 * 512 * 192 * 128
+
+
+def tile_scatter_matmul_kernel(tc, base, x, w, b, offs, out):
+    nc = tc.nc
+    sequences, features, tokens = base.shape
+    contraction, entries = x.shape
+    blocks = contraction // P
+    piece = entries // sequences
+    piece_cols = piece // 16
+    assert features == P and piece_cols % 2 == 0
+
+    with (
+        tc.tile_pool(name="held", bufs=1) as held,
+        tc.psum_pool(name="windows", bufs=1) as windows,
+    ):
+        base_sb = held.tile([P, sequences, tokens], BF16, name="base_sb")
+        w_sb = held.tile([P, blocks, features], BF16, name="w_sb")
+        x_sb = held.tile([P, blocks, entries], BF16, name="x_sb")
+        offsets = held.tile([P, entries // 16], U16, name="offsets")
+        bias = held.tile([P, 1], F32, name="bias")
+        ident = held.tile([P, P], BF16, name="ident")
+
+        nc.sync.dma_start(base_sb[:], base.rearrange("i m t -> m i t"))
+        nc.sync.dma_start(w_sb[:], w.rearrange("(p c) m -> p c m", c=blocks))
+        nc.sync.dma_start(x_sb[:], x.rearrange("(p c) n -> p c n", c=blocks))
+        nc.sync.dma_start(offsets[:], offs)
+        nc.scalar.dma_start(bias[:], b)
+
+        make_identity(nc, ident[:])
+
+        window = [windows.tile([P, tokens], F32, name=f"window_{i}") for i in range(sequences)]
+        for i in range(sequences):
+            nc.tensor.matmul(window[i][:], ident[:], base_sb[:, i, :], start=True, stop=False)
+
+        for i in range(sequences):
+            places = window[i][:].indirect(offsets[:, i * piece_cols : (i + 1) * piece_cols])
+            for c in range(blocks):
+                nc.tensor.matmul(
+                    places,
+                    w_sb[:, c, :],
+                    x_sb[:, c, i * piece : (i + 1) * piece],
+                    start=False,
+                    stop=c == blocks - 1,
+                )
+
+        for i, queue in enumerate((nc.sync, nc.scalar)):
+            result = held.tile([P, tokens], F32, name=f"result_{i}")
+            nc.vector.tensor_scalar(
+                result[:], window[i][:], bias[:, 0:1], 0.0, mybir.AluOpType.add, mybir.AluOpType.max
+            )
+            queue.dma_start(out[i], result[:])

@@ -6,6 +6,8 @@ F32 = mybir.dt.float32
 U16 = mybir.dt.uint16
 
 P = 128
+BANK_COLS = 512
+WARM_UP = 4
 FLOPS = 2 * 512 * 192 * 128
 
 
@@ -34,6 +36,12 @@ def tile_scatter_matmul_kernel(tc, base, x, w, b, offs, out):
         nc.sync.dma_start(x_sb[:], x.rearrange("(p c) n -> p c n", c=blocks))
         nc.sync.dma_start(offsets[:], offs)
         nc.scalar.dma_start(bias[:], b)
+
+        zeros = held.tile([P, BANK_COLS], BF16, name="zeros")
+        nc.vector.memset(zeros[:], 0.0)
+        spare = windows.tile([P, BANK_COLS], F32, name="spare")
+        for i in range(WARM_UP):
+            nc.tensor.matmul(spare[:], zeros[:, 0:P], zeros[:], start=True, stop=True)
 
         make_identity(nc, ident[:])
 

@@ -35,7 +35,7 @@ def tile_scatter_matmul_kernel(tc, base, x, w, b, offs, out):
         nc.sync.dma_start(w_sb[:], w.rearrange("(p c) m -> p c m", c=blocks))
         nc.sync.dma_start(x_sb[:], x.rearrange("(p c) n -> p c n", c=blocks))
         nc.sync.dma_start(offsets[:], offs)
-        nc.scalar.dma_start(bias[:], b)
+        nc.sync.dma_start(bias[:], b)
 
         zeros = held.tile([P, BANK_COLS], BF16, name="zeros")
         nc.vector.memset(zeros[:], 0.0)

@@ -6,8 +6,8 @@ F32 = mybir.dt.float32
 U16 = mybir.dt.uint16
 
 P = 128
-BANK_COLS = 512
-WARM_UP = 4
+WARM_COLS = 128
+WARM_UP = 16
 FLOPS = 2 * 512 * 192 * 128
 
 
@@ -37,9 +37,9 @@ def tile_scatter_matmul_kernel(tc, base, x, w, b, offs, out):
         nc.sync.dma_start(offsets[:], offs)
         nc.sync.dma_start(bias[:], b)
 
-        zeros = held.tile([P, BANK_COLS], BF16, name="zeros")
-        nc.vector.memset(zeros[:], 0.0)
-        spare = windows.tile([P, BANK_COLS], F32, name="spare")
+        zeros = held.tile([P, WARM_COLS], BF16, name="zeros")
+        nc.gpsimd.memset(zeros[:], 0.0)
+        spare = windows.tile([P, WARM_COLS], F32, name="spare")
         for i in range(WARM_UP):
             nc.tensor.matmul(spare[:], zeros[:, 0:P], zeros[:], start=True, stop=True)
 

from concourse.masks import make_identity
import concourse.mybir as mybir

BF16 = mybir.dt.bfloat16
F32 = mybir.dt.float32
U16 = mybir.dt.uint16

P = 128
WARM_COLS = 128
WARM_UP = 16
FLOPS = 2 * 512 * 192 * 128


def tile_scatter_matmul_kernel(tc, base, x, w, b, offs, out):
    nc = tc.nc
    sequences, features, tokens = base.shape
    contraction, entries = x.shape
    blocks = contraction // P
    piece = entries // sequences
    piece_cols = piece // 16
    assert features == P and piece_cols % 2 == 0

    with (
        tc.tile_pool(name="held", bufs=1) as held,
        tc.psum_pool(name="windows", bufs=1) as windows,
    ):
        base_sb = held.tile([P, sequences, tokens], BF16, name="base_sb")
        w_sb = held.tile([P, blocks, features], BF16, name="w_sb")
        x_sb = held.tile([P, blocks, entries], BF16, name="x_sb")
        offsets = held.tile([P, entries // 16], U16, name="offsets")
        bias = held.tile([P, 1], F32, name="bias")
        ident = held.tile([P, P], BF16, name="ident")

        nc.sync.dma_start(base_sb[:], base.rearrange("i m t -> m i t"))
        nc.sync.dma_start(w_sb[:], w.rearrange("(p c) m -> p c m", c=blocks))
        nc.sync.dma_start(x_sb[:], x.rearrange("(p c) n -> p c n", c=blocks))
        nc.sync.dma_start(offsets[:], offs)
        nc.sync.dma_start(bias[:], b)

        zeros = held.tile([P, WARM_COLS], BF16, name="zeros")
        nc.gpsimd.memset(zeros[:], 0.0)
        spare = windows.tile([P, WARM_COLS], F32, name="spare")
        for i in range(WARM_UP):
            nc.tensor.matmul(spare[:], zeros[:, 0:P], zeros[:], start=True, stop=True)

        make_identity(nc, ident[:])

        window = [windows.tile([P, tokens], F32, name=f"window_{i}") for i in range(sequences)]
        for i in range(sequences):
            nc.tensor.matmul(window[i][:], ident[:], base_sb[:, i, :], start=True, stop=False)

        for i in range(sequences):
            places = window[i][:].indirect(offsets[:, i * piece_cols : (i + 1) * piece_cols])
            for c in range(blocks):
                nc.tensor.matmul(
                    places,
                    w_sb[:, c, :],
                    x_sb[:, c, i * piece : (i + 1) * piece],
                    start=False,
                    stop=c == blocks - 1,
                )

        for i, queue in enumerate((nc.sync, nc.scalar)):
            result = held.tile([P, tokens], F32, name=f"result_{i}")
            nc.vector.tensor_scalar(
                result[:], window[i][:], bias[:, 0:1], 0.0, mybir.AluOpType.add, mybir.AluOpType.max
            )
            queue.dma_start(out[i], result[:])
